import numpy as np
import ml_dtypes


def mxq(x, axis, fmt="e4m3"):
    dtype, down = {"e4m3": (ml_dtypes.float8_e4m3fn, 7), "e5m2": (ml_dtypes.float8_e5m2, 14)}[fmt]
    v = np.moveaxis(np.asarray(x, np.float32).astype(ml_dtypes.bfloat16).astype(np.float64), axis, -1)
    blocks = v.reshape(v.shape[:-1] + (-1, 32))
    amax = np.abs(blocks).max(-1, keepdims=True)
    byte = np.maximum(np.where(amax > 0, np.frexp(amax)[1] - 1 + 127, 0) - down, 1)
    scale = np.exp2(byte - 127.0)
    codes = (blocks / scale).astype(np.float32).astype(dtype).astype(np.float64)
    return np.moveaxis((codes * scale).reshape(v.shape), -1, axis)


WIDE = False


def mx_kscale(k):
    if not WIDE:
        return np.ones(k)
    levels = np.array([10, -10, 5, -5, 0])
    if k % 512:
        return np.exp2(np.random.permutation(np.resize(levels, k // 32))).repeat(32)
    a = np.empty((k // 512, 16))
    for p in range(k // 512):
        a[p, :8] = np.random.permutation(np.resize(levels, 8))
        for g in range(8):
            far = levels[np.abs(levels - a[p, g]) >= 10]
            a[p, g + 8] = far[np.random.randint(len(far))]
    return np.exp2(a.ravel()).repeat(32)


def f64(x):
    return np.asarray(x).astype(np.float64)


def striped(idx):
    return np.tile(idx.reshape(-1, 16).T, (8, 1)).astype(np.uint16)


def unstriped(offs):
    return offs[:16].T.reshape(-1).astype(np.int64)


def pack_weight(w):
    k, n = w.shape
    w = f64(np.asarray(w, np.float32).astype(ml_dtypes.bfloat16)).reshape(k // 32, 32, n)
    amax = np.abs(w).max(1)
    byte = np.clip(np.where(amax > 0, np.frexp(amax)[1] - 1 + 127 - 7, 1), 1, 254)
    scaled = (w * np.exp2(127.0 - byte)[:, None, :]).reshape(k, n).astype(np.float32)
    words = np.ascontiguousarray(scaled.reshape(k // 512, 128, 4, n).transpose(0, 1, 3, 2)).astype(ml_dtypes.float8_e4m3fn).view(np.uint8)
    return words, np.ascontiguousarray(byte.astype(np.uint8).reshape(k // 512, 16, n))


def unpack_weight(words, scales):
    g, p, n, _ = words.shape
    vals = np.ascontiguousarray(words).view(ml_dtypes.float8_e4m3fn).astype(np.float64) * np.repeat(np.exp2(scales.astype(np.float64) - 127.0), 8, axis=1)[..., None]
    return vals.transpose(0, 1, 3, 2).reshape(g * 512, n)


def relu(v):
    return np.maximum(v, 0.0)


def sigmoid(v):
    return 1.0 / (1.0 + np.exp(-np.maximum(v, -700.0)))


K, T, S, D, H, V, Z, W = 512, 2048, 512, 2, 512, 256, 512, 2048
P = 2 ** 7


def setup_inputs():
    n = np.random.standard_normal
    s = mx_kscale(K)[:, None]
    packed_xT = pack_weight(n((K, T)) * s)
    packed_eT = pack_weight(n((K, W)) * s)
    return {
        "x_words": packed_xT[0],
        "x_scales": packed_xT[1],
        "w1": (n((K, H)) / np.sqrt(K) / s).astype(np.float32),
        "w2": (n((K, H)) / np.sqrt(K) / s).astype(np.float32),
        "e_words": packed_eT[0],
        "e_scales": packed_eT[1],
        "unit": (np.random.uniform(0.6, 1.4, (K, 1)) / np.sqrt(K) / s).astype(np.float32),
        "prior": (np.tile(np.random.uniform(0.05, 0.9, W), (P, 1))).astype(np.float32),
        "offs": striped(np.random.permutation(T)[:S]),
        "ent": striped(np.random.permutation(W)[:Z]),
        "cor": striped(np.random.permutation(V)),
    }


def reference(x_words, x_scales, w1, w2, e_words, e_scales, unit, prior, offs, ent, cor):
    xq = unpack_weight(x_words, x_scales)[:, unstriped(offs)]
    y = mxq(f64(w1), 0, "e4m3").T @ xq
    yw = mxq(f64(w2), 0, "e4m3").T @ xq
    yr = relu(y) - (0.5 * yw)
    ment = yr.reshape(len(yr), -1, D).max(axis=2)
    coh = ment * (sigmoid(ment[:, unstriped(cor)]))
    hid = f64(unit) * coh
    e_ent = unpack_weight(e_words, e_scales)[:, unstriped(ent)]
    sc = mxq(hid, 0, "e4m3").T @ e_ent
    lp = sc + np.log(f64(prior)[:1][:, unstriped(ent)])
    el = np.exp(2.0 * np.tanh(lp))
    lse = np.log(el.mean(axis=1, keepdims=True) + 0.05)
    over = relu(lp - lse)
    return over * sc

@@ -1,0 +1,230 @@
+import math
+from contextlib import ExitStack
+
+import concourse.mybir as mybir
+from concourse.masks import make_identity
+
+F32 = mybir.dt.float32
+BF16 = mybir.dt.bfloat16
+U32 = mybir.dt.uint32
+I32 = mybir.dt.int32
+U16 = mybir.dt.uint16
+U8 = mybir.dt.uint8
+FP8X4 = mybir.dt.float8_e4m3fn_x4
+ALU = mybir.AluOpType
+ACT = mybir.ActivationFunctionType
+
+P = 128
+PACK = 4
+K, T, S, H, V, Z = 512, 2048, 512, 512, 256, 512
+FLOPS = 2 * K * H * S * 2 + 2 * H * V * Z
+
+TERMS = 256
+A_LOW = math.exp(-2.0) + 0.05
+A_HIGH = math.exp(2.0) + 0.05
+CENTRE = 0.5 * (A_LOW + A_HIGH)
+
+
+def load_scale_rows(queue, plane, rows):
+    for q in range(4):
+        queue.dma_start(out=plane[32 * q : 32 * q + 4, :].bitcast(I32), in_=rows[0, 4 * q : 4 * q + 4, :].bitcast(I32))
+
+
+def tile_picked_yentity_over_p_kernel(
+    tc, x_words, x_scales, w1, w2, e_words, e_scales, unit, prior, offs, ent, cor, out
+):
+    nc = tc.nc
+    with ExitStack() as ctx:
+        sb = ctx.enter_context(tc.tile_pool(name="sb", bufs=1))
+        ps = ctx.enter_context(tc.psum_pool(name="ps", bufs=1))
+
+        offs_t = sb.tile([P, S // 16], U16, name="offs_t")
+        ent_t = sb.tile([P, Z // 16], U16, name="ent_t")
+        cor_t = sb.tile([P, V // 16], U16, name="cor_t")
+        x_tab = sb.tile([P, T], U32, name="x_tab")
+        e_tab = sb.tile([P, T], U32, name="e_tab")
+        xs_tab = sb.tile([P, T], U8, name="xs_tab")
+        es_tab = sb.tile([P, T], U8, name="es_tab")
+        w_raw = [[sb.tile([P, PACK, H // 2], F32, name="w_raw%d%d" % (n, a)) for a in range(2)] for n in range(2)]
+        prior_col = sb.tile([P, T // P], F32, name="prior_col")
+        unit_t = sb.tile([P, PACK], F32, name="unit_t")
+        ident = sb.tile([P, P], F32, name="ident")
+        counts = sb.tile([P, TERMS + 1], F32, name="counts")
+        coefs = sb.tile([P, TERMS + 1], F32, name="coefs")
+
+        nc.vector.memset(xs_tab[:].bitcast(I32), 0)
+        nc.vector.memset(es_tab[:].bitcast(I32), 0)
+        nc.gpsimd.iota(counts[:], [[-1, TERMS + 1]], base=TERMS, channel_multiplier=0, allow_small_or_imprecise_dtypes=True)
+        make_identity(nc, ident[:])
+
+        def load_weights(n, a, j0, j1):
+            rows = (w1, w2)[n].rearrange("(p j) c -> p j c", j=PACK)
+            nc.sync.dma_start(out=w_raw[n][a][:, j0:j1, :], in_=rows[:, j0:j1, a * (H // 2) : (a + 1) * (H // 2)])
+
+        nc.sync.dma_start(out=prior_col[:], in_=prior[0, :].rearrange("(n b) -> n b", b=T // P))
+        nc.sync.dma_start(offs_t[:], offs)
+        nc.sync.dma_start(ent_t[:], ent)
+        nc.sync.dma_start(cor_t[:], cor)
+        nc.sync.dma_start(out=unit_t[:], in_=unit.rearrange("(p t) o -> p (t o)", t=PACK))
+        load_weights(0, 0, 0, 2)
+        load_weights(0, 0, 2, 4)
+        load_weights(0, 1, 0, 4)
+        load_scale_rows(nc.sync, xs_tab, x_scales)
+        nc.sync.dma_start(out=x_tab[:].bitcast(I32), in_=x_words[0].rearrange("p n r -> p (n r)").bitcast(I32))
+        load_scale_rows(nc.sync, es_tab, e_scales)
+        load_weights(1, 0, 0, 4)
+        load_weights(1, 1, 0, 4)
+        nc.sync.dma_start(out=e_tab[:].bitcast(I32), in_=e_words[0].rearrange("p n r -> p (n r)").bitcast(I32))
+
+        nc.vector.reciprocal(coefs[:, 0:TERMS], counts[:, 0:TERMS])
+        nc.vector.tensor_scalar(
+            coefs[:, TERMS : TERMS + 1], counts[:, TERMS : TERMS + 1], -math.log(CENTRE), None, ALU.add
+        )
+
+        log_prior = sb.tile([P, T], F32, name="log_prior")
+        log_prior_v = log_prior[:].rearrange("p (n b) -> p n b", b=T // P)
+        for q in range(4):
+            spread = ps.tile([P, 4, P], F32, name="spread%d" % q, tag="bank_a%d" % q)
+            for i in range(4):
+                b = 4 * q + i
+                nc.tensor.transpose(spread[:, i, :], prior_col[:, b : b + 1].to_broadcast([P, P]), ident[:])
+            nc.scalar.activation(
+                log_prior_v[:, :, 4 * q : 4 * q + 4], spread[:].rearrange("p i n -> p n i"), ACT.Ln
+            )
+
+        x_codes = sb.tile([P, S], U32, name="x_codes", align_bytes=64)
+        x_bytes = sb.tile([P, S], U8, name="x_bytes", align_bytes=64)
+        e_bytes = sb.tile([P, Z], U8, name="e_bytes", align_bytes=64)
+        w_bf = [sb.tile([P, PACK, P, PACK], BF16, name="w_bf%d" % n, align_bytes=64) for n in range(2)]
+        w_codes = [sb.tile([P, H], U32, name="w_codes%d" % n, align_bytes=64) for n in range(2)]
+        w_bytes = [sb.tile([P, H], U8, name="w_bytes%d" % n, align_bytes=64) for n in range(2)]
+
+        def deal(copy, n, a):
+            copy(
+                out=w_bf[n][:, :, a * (P // 2) : (a + 1) * (P // 2), :].rearrange("p t m j -> p m j t"),
+                in_=w_raw[n][a][:].rearrange("p j (m t) -> p m j t", t=PACK),
+            )
+
+        def quantize_weights(n, t):
+            cols = slice(t * P, (t + 1) * P)
+            nc.vector.quantize_mx(
+                out=w_codes[n][:, cols].bitcast(FP8X4),
+                scales=w_bytes[n][:, cols],
+                in_=w_bf[n][:, t].rearrange("p m j -> p (m j)"),
+            )
+
+        def first_product(n, t, bank):
+            cols = slice(t * P, (t + 1) * P)
+            nc.tensor.matmul_mx(
+                out=bank[:],
+                lhsT=w_codes[n][:, cols].bitcast(FP8X4),
+                lhsT_scale=w_bytes[n][:, cols],
+                rhs=x_codes[:].bitcast(FP8X4),
+                rhs_scale=x_bytes[:],
+                start=True,
+                stop=True,
+            )
+
+        ent_prior = sb.tile([P, Z], F32, name="ent_prior")
+        nc.scalar.activation(ent_prior[:], log_prior[:].indirect(ent_t[:]), ACT.Copy)
+        deal(nc.vector.tensor_copy, 0, 0)
+        deal(nc.vector.tensor_copy, 0, 1)
+        for t in range(PACK):
+            quantize_weights(0, t)
+        nc.vector.tensor_copy(x_bytes[:], xs_tab[:].indirect(offs_t[:]))
+        nc.vector.tensor_copy(x_codes[:], x_tab[:].indirect(offs_t[:]))
+        nc.vector.tensor_copy(e_bytes[:], es_tab[:].indirect(ent_t[:]))
+        deal(nc.scalar.copy, 1, 0)
+        relu_y = [sb.tile([P, S], F32, name="relu_y%d" % t) for t in range(PACK)]
+        for t in range(PACK):
+            y = ps.tile([P, S], F32, name="y%d" % t, tag="bank_a%d" % t)
+            first_product(0, t, y)
+            nc.scalar.activation(relu_y[t][:], y[:], ACT.Relu)
+        deal(nc.vector.tensor_copy, 1, 1)
+        yw = []
+        for t in range(PACK):
+            quantize_weights(1, t)
+            bank = ps.tile([P, S], F32, name="yw%d" % t, tag="bank_b%d" % t)
+            first_product(1, t, bank)
+            yw.append(bank)
+
+        yr = [sb.tile([P, V, 2], F32, name="yr%d" % t, tag="yr%d" % t, align_bytes=64) for t in range(PACK)]
+        ment = [sb.tile([P, V], F32, name="ment%d" % t) for t in range(PACK)]
+        gate = sb.tile([P, PACK, V], F32, name="gate")
+        scaled = sb.tile([P, PACK, V], F32, name="scaled")
+
+        def difference(t):
+            nc.vector.scalar_tensor_tensor(
+                yr[t][:].rearrange("p v d -> p (v d)"), yw[t][:], -0.5, relu_y[t][:], ALU.mult, ALU.add
+            )
+
+        def mention(t):
+            nc.vector.tensor_tensor(ment[t][:], yr[t][:, :, 0], yr[t][:, :, 1], ALU.max)
+            for h in range(2):
+                nc.scalar.activation(
+                    gate[:, t, h * P : (h + 1) * P], ment[t][:].indirect(cor_t[:, h * 8 : (h + 1) * 8]), ACT.Sigmoid
+                )
+            if t % 2 == 0:
+                nc.scalar.activation(scaled[:, t, :], ment[t][:], ACT.Copy, scale=unit_t[:, t : t + 1])
+            else:
+                nc.vector.tensor_scalar(scaled[:, t, :], ment[t][:], unit_t[:, t : t + 1], None, ALU.mult)
+
+        difference(0)
+        for t in range(1, PACK):
+            difference(t)
+            mention(t - 1)
+        mention(PACK - 1)
+        e_codes = sb.tile([P, Z], U32, name="e_codes", tag="yr%d" % (PACK - 1), align_bytes=64)
+        nc.vector.tensor_copy(e_codes[:], e_tab[:].indirect(ent_t[:]))
+
+        sc, lp = [], []
+        for h in range(2):
+            rows = slice(h * P, (h + 1) * P)
+            hid = sb.tile([P, P, PACK], BF16, name="hid%d" % h, align_bytes=64)
+            nc.vector.tensor_tensor(
+                hid[:].rearrange("p (c i) t -> p c t i", i=4),
+                gate[:, :, rows].rearrange("p t (c i) -> p c t i", i=4),
+                scaled[:, :, rows].rearrange("p t (c i) -> p c t i", i=4),
+                ALU.mult,
+            )
+            hid_codes = sb.tile([P, P], U32, name="hid_codes%d" % h, align_bytes=64)
+            hid_bytes = sb.tile([P, P], U8, name="hid_bytes%d" % h, align_bytes=64)
+            nc.vector.quantize_mx(
+                out=hid_codes[:].bitcast(FP8X4), scales=hid_bytes[:], in_=hid[:].rearrange("p v t -> p (v t)")
+            )
+            bank = ps.tile([P, Z], F32, name="sc%d" % h, tag="bank_a%d" % h)
+            nc.tensor.matmul_mx(
+                out=bank[:],
+                lhsT=hid_codes[:].bitcast(FP8X4),
+                lhsT_scale=hid_bytes[:],
+                rhs=e_codes[:].bitcast(FP8X4),
+                rhs_scale=e_bytes[:],
+                start=True,
+                stop=True,
+            )
+            sc.append(bank)
+            lp.append(sb.tile([P, Z], F32, name="lp%d" % h))
+        for h in range(2):
+            nc.vector.tensor_tensor(lp[h][:], sc[h][:], ent_prior[:], ALU.add)
+
+        for h in range(2):
+            rows = slice(h * P, (h + 1) * P)
+            squashed = sb.tile([P, Z], F32, name="squashed%d" % h)
+            el = sb.tile([P, Z], F32, name="el%d" % h)
+            total = sb.tile([P, 1], F32, name="total%d" % h)
+            below = sb.tile([P, 1], F32, name="below%d" % h)
+            series = sb.tile([P, TERMS + 1], F32, name="series%d" % h)
+            over = sb.tile([P, Z], F32, name="over%d" % h)
+            result = sb.tile([P, Z], F32, name="result%d" % h)
+            nc.scalar.activation(squashed[:], lp[h][:], ACT.Tanh)
+            nc.scalar.activation(el[:], squashed[:], ACT.Exp, scale=2.0, accum_out=total[:])
+            if h == 0:
+                nc.vector.tensor_scalar(below[:], total[:], -1.0 / (Z * CENTRE), 1.0 - 0.05 / CENTRE, ALU.mult, ALU.add)
+            else:
+                nc.scalar.activation(below[:], total[:], ACT.Copy, scale=-1.0 / (Z * CENTRE), bias=1.0 - 0.05 / CENTRE)
+            nc.vector.tensor_tensor_scan(
+                series[:], below[:].to_broadcast([P, TERMS + 1]), coefs[:], 0.0, ALU.mult, ALU.add
+            )
+            nc.vector.tensor_scalar(over[:], lp[h][:], series[:, TERMS : TERMS + 1], 0.0, ALU.add, ALU.max)
+            nc.vector.tensor_tensor(result[:], sc[h][:], over[:], ALU.mult)
+            nc.sync.dma_start(out=out[rows, :], in_=result[:])

@@ -19,7 +19,7 @@ PACK = 4
 K, T, S, H, V, Z = 512, 2048, 512, 512, 256, 512
 FLOPS = 2 * K * H * S * 2 + 2 * H * V * Z
 
-TERMS = 256
+TERMS = 192
 A_LOW = math.exp(-2.0) + 0.05
 A_HIGH = math.exp(2.0) + 0.05
 CENTRE = 0.5 * (A_LOW + A_HIGH)
@@ -41,16 +41,16 @@ def tile_picked_yentity_over_p_kernel(
         offs_t = sb.tile([P, S // 16], U16, name="offs_t")
         ent_t = sb.tile([P, Z // 16], U16, name="ent_t")
         cor_t = sb.tile([P, V // 16], U16, name="cor_t")
-        x_tab = sb.tile([P, T], U32, name="x_tab")
+        x_tab = sb.tile([P, T], U32, name="x_tab", tag="x_tab", align_bytes=64)
         e_tab = sb.tile([P, T], U32, name="e_tab")
         xs_tab = sb.tile([P, T], U8, name="xs_tab")
         es_tab = sb.tile([P, T], U8, name="es_tab")
-        w_raw = [[sb.tile([P, PACK, H // 2], F32, name="w_raw%d%d" % (n, a)) for a in range(2)] for n in range(2)]
+        w_raw = [[sb.tile([P, PACK, H // 2], F32, name="w_raw%d%d" % (n, a), tag="w_raw%d%d" % (n, a)) for a in range(2)] for n in range(2)]
         prior_col = sb.tile([P, T // P], F32, name="prior_col")
         unit_t = sb.tile([P, PACK], F32, name="unit_t")
         ident = sb.tile([P, P], F32, name="ident")
         counts = sb.tile([P, TERMS + 1], F32, name="counts")
-        coefs = sb.tile([P, TERMS + 1], F32, name="coefs")
+        log_counts = sb.tile([P, TERMS], F32, name="log_counts")
 
         nc.vector.memset(xs_tab[:].bitcast(I32), 0)
         nc.vector.memset(es_tab[:].bitcast(I32), 0)
@@ -76,10 +76,7 @@ def tile_picked_yentity_over_p_kernel(
         load_weights(1, 1, 0, 4)
         nc.sync.dma_start(out=e_tab[:].bitcast(I32), in_=e_words[0].rearrange("p n r -> p (n r)").bitcast(I32))
 
-        nc.vector.reciprocal(coefs[:, 0:TERMS], counts[:, 0:TERMS])
-        nc.vector.tensor_scalar(
-            coefs[:, TERMS : TERMS + 1], counts[:, TERMS : TERMS + 1], -math.log(CENTRE), None, ALU.add
-        )
+        nc.scalar.activation(log_counts[:], counts[:, 0:TERMS], ACT.Ln)
 
         log_prior = sb.tile([P, T], F32, name="log_prior")
         log_prior_v = log_prior[:].rearrange("p (n b) -> p n b", b=T // P)
@@ -94,7 +91,6 @@ def tile_picked_yentity_over_p_kernel(
 
         x_codes = sb.tile([P, S], U32, name="x_codes", align_bytes=64)
         x_bytes = sb.tile([P, S], U8, name="x_bytes", align_bytes=64)
-        e_bytes = sb.tile([P, Z], U8, name="e_bytes", align_bytes=64)
         w_bf = [sb.tile([P, PACK, P, PACK], BF16, name="w_bf%d" % n, align_bytes=64) for n in range(2)]
         w_codes = [sb.tile([P, H], U32, name="w_codes%d" % n, align_bytes=64) for n in range(2)]
         w_bytes = [sb.tile([P, H], U8, name="w_bytes%d" % n, align_bytes=64) for n in range(2)]
@@ -133,13 +129,14 @@ def tile_picked_yentity_over_p_kernel(
             quantize_weights(0, t)
         nc.vector.tensor_copy(x_bytes[:], xs_tab[:].indirect(offs_t[:]))
         nc.vector.tensor_copy(x_codes[:], x_tab[:].indirect(offs_t[:]))
+        e_bytes = sb.tile([P, Z], U8, name="e_bytes", tag="x_tab", align_bytes=64)
         nc.vector.tensor_copy(e_bytes[:], es_tab[:].indirect(ent_t[:]))
         deal(nc.scalar.copy, 1, 0)
-        relu_y = [sb.tile([P, S], F32, name="relu_y%d" % t) for t in range(PACK)]
+        relu_y = sb.tile([P, PACK, S], F32, name="relu_y", tag="w_raw10")
         for t in range(PACK):
             y = ps.tile([P, S], F32, name="y%d" % t, tag="bank_a%d" % t)
             first_product(0, t, y)
-            nc.scalar.activation(relu_y[t][:], y[:], ACT.Relu)
+            nc.scalar.activation(relu_y[:, t, :], y[:], ACT.Relu)
         deal(nc.vector.tensor_copy, 1, 1)
         yw = []
         for t in range(PACK):
@@ -149,13 +146,13 @@ def tile_picked_yentity_over_p_kernel(
             yw.append(bank)
 
         yr = [sb.tile([P, V, 2], F32, name="yr%d" % t, tag="yr%d" % t, align_bytes=64) for t in range(PACK)]
-        ment = [sb.tile([P, V], F32, name="ment%d" % t) for t in range(PACK)]
+        ment = [sb.tile([P, V], F32, name="ment%d" % t, tag="ment%d" % t) for t in range(PACK)]
         gate = sb.tile([P, PACK, V], F32, name="gate")
         scaled = sb.tile([P, PACK, V], F32, name="scaled")
 
         def difference(t):
             nc.vector.scalar_tensor_tensor(
-                yr[t][:].rearrange("p v d -> p (v d)"), yw[t][:], -0.5, relu_y[t][:], ALU.mult, ALU.add
+                yr[t][:].rearrange("p v d -> p (v d)"), yw[t][:], -0.5, relu_y[:, t, :], ALU.mult, ALU.add
             )
 
         def mention(t):
@@ -176,6 +173,11 @@ def tile_picked_yentity_over_p_kernel(
         mention(PACK - 1)
         e_codes = sb.tile([P, Z], U32, name="e_codes", tag="yr%d" % (PACK - 1), align_bytes=64)
         nc.vector.tensor_copy(e_codes[:], e_tab[:].indirect(ent_t[:]))
+        coefs = sb.tile([P, TERMS + 1], F32, name="coefs", tag="ment%d" % (PACK - 1))
+        nc.scalar.activation(coefs[:, 0:TERMS], log_counts[:], ACT.Exp, scale=-1.0)
+        nc.gpsimd.tensor_scalar(
+            coefs[:, TERMS : TERMS + 1], counts[:, TERMS : TERMS + 1], 1.0, -math.log(CENTRE), ALU.mult, ALU.add
+        )
 
         sc, lp = [], []
         for h in range(2):
@@ -225,6 +227,15 @@ def tile_picked_yentity_over_p_kernel(
             nc.vector.tensor_tensor_scan(
                 series[:], below[:].to_broadcast([P, TERMS + 1]), coefs[:], 0.0, ALU.mult, ALU.add
             )
-            nc.vector.tensor_scalar(over[:], lp[h][:], series[:, TERMS : TERMS + 1], 0.0, ALU.add, ALU.max)
-            nc.vector.tensor_tensor(result[:], sc[h][:], over[:], ALU.mult)
-            nc.sync.dma_start(out=out[rows, :], in_=result[:])
+            minus_lse = series[:, TERMS : TERMS + 1]
+            if h == 0:
+                nc.vector.tensor_scalar(over[:], lp[h][:], minus_lse, 0.0, ALU.add, ALU.max)
+                nc.vector.tensor_tensor(result[:], sc[h][:], over[:], ALU.mult)
+                nc.sync.dma_start(out=out[rows, :], in_=result[:])
+            else:
+                left, right = slice(0, Z // 2), slice(Z // 2, Z)
+                nc.vector.tensor_scalar(over[:, left], lp[h][:, left], minus_lse, 0.0, ALU.add, ALU.max)
+                nc.scalar.activation(over[:, right], lp[h][:, right], ACT.Relu, bias=minus_lse)
+                for cols, queue in ((left, nc.sync), (right, nc.scalar)):
+                    nc.vector.tensor_tensor(result[:, cols], sc[h][:, cols], over[:, cols], ALU.mult)
+                    queue.dma_start(out=out[rows, cols], in_=result[:, cols])

@@ -26,8 +26,8 @@ CENTRE = 0.5 * (A_LOW + A_HIGH)
 
 
 def load_scale_rows(queue, plane, rows):
-    for q in range(4):
-        queue.dma_start(out=plane[32 * q : 32 * q + 4, :].bitcast(I32), in_=rows[0, 4 * q : 4 * q + 4, :].bitcast(I32))
+    for r in range(4):
+        queue.dma_start(out=plane[r:P:32, :].bitcast(I32), in_=rows[0, r:16:4, :].bitcast(I32))
 
 
 def tile_picked_yentity_over_p_kernel(
@@ -45,7 +45,8 @@ def tile_picked_yentity_over_p_kernel(
         e_tab = sb.tile([P, T], U32, name="e_tab")
         xs_tab = sb.tile([P, T], U8, name="xs_tab")
         es_tab = sb.tile([P, T], U8, name="es_tab")
-        w_raw = [[sb.tile([P, PACK, H // 2], F32, name="w_raw%d%d" % (n, a), tag="w_raw%d%d" % (n, a)) for a in range(2)] for n in range(2)]
+        w1_raw = sb.tile([P, PACK, H], F32, name="w1_raw")
+        w2_raw = [sb.tile([P, PACK, H // 2], F32, name="w2_raw%d" % a, tag="w2_raw%d" % a) for a in range(2)]
         prior_col = sb.tile([P, T // P], F32, name="prior_col")
         unit_t = sb.tile([P, PACK], F32, name="unit_t")
         ident = sb.tile([P, P], F32, name="ident")
@@ -57,23 +58,20 @@ def tile_picked_yentity_over_p_kernel(
         nc.gpsimd.iota(counts[:], [[-1, TERMS + 1]], base=TERMS, channel_multiplier=0, allow_small_or_imprecise_dtypes=True)
         make_identity(nc, ident[:])
 
-        def load_weights(n, a, j0, j1):
-            rows = (w1, w2)[n].rearrange("(p j) c -> p j c", j=PACK)
-            nc.sync.dma_start(out=w_raw[n][a][:, j0:j1, :], in_=rows[:, j0:j1, a * (H // 2) : (a + 1) * (H // 2)])
-
+        w1_rows = w1.rearrange("(p j) c -> p j c", j=PACK)
+        w2_rows = w2.rearrange("(p j) c -> p j c", j=PACK)
         nc.sync.dma_start(out=prior_col[:], in_=prior[0, :].rearrange("(n b) -> n b", b=T // P))
         nc.sync.dma_start(offs_t[:], offs)
         nc.sync.dma_start(ent_t[:], ent)
         nc.sync.dma_start(cor_t[:], cor)
-        nc.sync.dma_start(out=unit_t[:], in_=unit.rearrange("(p t) o -> p (t o)", t=PACK))
-        load_weights(0, 0, 0, 2)
-        load_weights(0, 0, 2, 4)
-        load_weights(0, 1, 0, 4)
+        for j in range(PACK):
+            nc.sync.dma_start(out=w1_raw[:, j, :], in_=w1_rows[:, j, :])
         load_scale_rows(nc.sync, xs_tab, x_scales)
         nc.sync.dma_start(out=x_tab[:].bitcast(I32), in_=x_words[0].rearrange("p n r -> p (n r)").bitcast(I32))
         load_scale_rows(nc.sync, es_tab, e_scales)
-        load_weights(1, 0, 0, 4)
-        load_weights(1, 1, 0, 4)
+        for a in range(2):
+            nc.sync.dma_start(out=w2_raw[a][:], in_=w2_rows[:, :, a * (H // 2) : (a + 1) * (H // 2)])
+        nc.sync.dma_start(out=unit_t[:], in_=unit.rearrange("(p t) o -> p (t o)", t=PACK))
         nc.sync.dma_start(out=e_tab[:].bitcast(I32), in_=e_words[0].rearrange("p n r -> p (n r)").bitcast(I32))
 
         nc.scalar.activation(log_counts[:], counts[:, 0:TERMS], ACT.Ln)
@@ -95,11 +93,8 @@ def tile_picked_yentity_over_p_kernel(
         w_codes = [sb.tile([P, H], U32, name="w_codes%d" % n, align_bytes=64) for n in range(2)]
         w_bytes = [sb.tile([P, H], U8, name="w_bytes%d" % n, align_bytes=64) for n in range(2)]
 
-        def deal(copy, n, a):
-            copy(
-                out=w_bf[n][:, :, a * (P // 2) : (a + 1) * (P // 2), :].rearrange("p t m j -> p m j t"),
-                in_=w_raw[n][a][:].rearrange("p j (m t) -> p m j t", t=PACK),
-            )
+        def deal(copy, dealt, raw):
+            copy(out=dealt.rearrange("p t m j -> p m j t"), in_=raw.rearrange("p j (m t) -> p m j t", t=PACK))
 
         def quantize_weights(n, t):
             cols = slice(t * P, (t + 1) * P)
@@ -123,21 +118,20 @@ def tile_picked_yentity_over_p_kernel(
 
         ent_prior = sb.tile([P, Z], F32, name="ent_prior")
         nc.scalar.activation(ent_prior[:], log_prior[:].indirect(ent_t[:]), ACT.Copy)
-        deal(nc.vector.tensor_copy, 0, 0)
-        deal(nc.vector.tensor_copy, 0, 1)
+        deal(nc.vector.tensor_copy, w_bf[0][:], w1_raw[:])
         for t in range(PACK):
             quantize_weights(0, t)
         nc.vector.tensor_copy(x_bytes[:], xs_tab[:].indirect(offs_t[:]))
         nc.vector.tensor_copy(x_codes[:], x_tab[:].indirect(offs_t[:]))
         e_bytes = sb.tile([P, Z], U8, name="e_bytes", tag="x_tab", align_bytes=64)
         nc.vector.tensor_copy(e_bytes[:], es_tab[:].indirect(ent_t[:]))
-        deal(nc.scalar.copy, 1, 0)
-        relu_y = sb.tile([P, PACK, S], F32, name="relu_y", tag="w_raw10")
+        deal(nc.scalar.copy, w_bf[1][:, :, 0 : P // 2, :], w2_raw[0][:])
+        relu_y = sb.tile([P, PACK, S], F32, name="relu_y", tag="w2_raw0")
         for t in range(PACK):
             y = ps.tile([P, S], F32, name="y%d" % t, tag="bank_a%d" % t)
             first_product(0, t, y)
             nc.scalar.activation(relu_y[:, t, :], y[:], ACT.Relu)
-        deal(nc.vector.tensor_copy, 1, 1)
+        deal(nc.vector.tensor_copy, w_bf[1][:, :, P // 2 : P, :], w2_raw[1][:])
         yw = []
         for t in range(PACK):
             quantize_weights(1, t)
@@ -161,10 +155,7 @@ def tile_picked_yentity_over_p_kernel(
                 nc.scalar.activation(
                     gate[:, t, h * P : (h + 1) * P], ment[t][:].indirect(cor_t[:, h * 8 : (h + 1) * 8]), ACT.Sigmoid
                 )
-            if t % 2 == 0:
-                nc.scalar.activation(scaled[:, t, :], ment[t][:], ACT.Copy, scale=unit_t[:, t : t + 1])
-            else:
-                nc.vector.tensor_scalar(scaled[:, t, :], ment[t][:], unit_t[:, t : t + 1], None, ALU.mult)
+            nc.gpsimd.tensor_scalar(scaled[:, t, :], ment[t][:], unit_t[:, t : t + 1], 0.0, ALU.mult, ALU.add)
 
         difference(0)
         for t in range(1, PACK):
@@ -179,24 +170,27 @@ def tile_picked_yentity_over_p_kernel(
             coefs[:, TERMS : TERMS + 1], counts[:, TERMS : TERMS + 1], 1.0, -math.log(CENTRE), ALU.mult, ALU.add
         )
 
-        sc, lp = [], []
-        for h in range(2):
+        hid = [sb.tile([P, P, PACK], BF16, name="hid%d" % h, align_bytes=64) for h in range(2)]
+        sc = [ps.tile([P, Z], F32, name="sc%d" % h, tag="bank_a%d" % h) for h in range(2)]
+        lp = [sb.tile([P, Z], F32, name="lp%d" % h) for h in range(2)]
+
+        def hidden(h):
             rows = slice(h * P, (h + 1) * P)
-            hid = sb.tile([P, P, PACK], BF16, name="hid%d" % h, align_bytes=64)
             nc.vector.tensor_tensor(
-                hid[:].rearrange("p (c i) t -> p c t i", i=4),
+                hid[h][:].rearrange("p (c i) t -> p c t i", i=4),
                 gate[:, :, rows].rearrange("p t (c i) -> p c t i", i=4),
                 scaled[:, :, rows].rearrange("p t (c i) -> p c t i", i=4),
                 ALU.mult,
             )
+
+        def second_product(h):
             hid_codes = sb.tile([P, P], U32, name="hid_codes%d" % h, align_bytes=64)
             hid_bytes = sb.tile([P, P], U8, name="hid_bytes%d" % h, align_bytes=64)
             nc.vector.quantize_mx(
-                out=hid_codes[:].bitcast(FP8X4), scales=hid_bytes[:], in_=hid[:].rearrange("p v t -> p (v t)")
+                out=hid_codes[:].bitcast(FP8X4), scales=hid_bytes[:], in_=hid[h][:].rearrange("p v t -> p (v t)")
             )
-            bank = ps.tile([P, Z], F32, name="sc%d" % h, tag="bank_a%d" % h)
             nc.tensor.matmul_mx(
-                out=bank[:],
+                out=sc[h][:],
                 lhsT=hid_codes[:].bitcast(FP8X4),
                 lhsT_scale=hid_bytes[:],
                 rhs=e_codes[:].bitcast(FP8X4),
@@ -204,10 +198,13 @@ def tile_picked_yentity_over_p_kernel(
                 start=True,
                 stop=True,
             )
-            sc.append(bank)
-            lp.append(sb.tile([P, Z], F32, name="lp%d" % h))
-        for h in range(2):
-            nc.vector.tensor_tensor(lp[h][:], sc[h][:], ent_prior[:], ALU.add)
+
+        hidden(0)
+        second_product(0)
+        hidden(1)
+        nc.vector.tensor_tensor(lp[0][:], sc[0][:], ent_prior[:], ALU.add)
+        second_product(1)
+        nc.vector.tensor_tensor(lp[1][:], sc[1][:], ent_prior[:], ALU.add)
 
         for h in range(2):
             rows = slice(h * P, (h + 1) * P)

import math
from contextlib import ExitStack

import concourse.mybir as mybir
from concourse.masks import make_identity

F32 = mybir.dt.float32
BF16 = mybir.dt.bfloat16
U32 = mybir.dt.uint32
I32 = mybir.dt.int32
U16 = mybir.dt.uint16
U8 = mybir.dt.uint8
FP8X4 = mybir.dt.float8_e4m3fn_x4
ALU = mybir.AluOpType
ACT = mybir.ActivationFunctionType

P = 128
PACK = 4
K, T, S, H, V, Z = 512, 2048, 512, 512, 256, 512
FLOPS = 2 * K * H * S * 2 + 2 * H * V * Z

TERMS = 192
A_LOW = math.exp(-2.0) + 0.05
A_HIGH = math.exp(2.0) + 0.05
CENTRE = 0.5 * (A_LOW + A_HIGH)


def load_scale_rows(queue, plane, rows):
    for r in range(4):
        queue.dma_start(out=plane[r:P:32, :].bitcast(I32), in_=rows[0, r:16:4, :].bitcast(I32))


def tile_picked_yentity_over_p_kernel(
    tc, x_words, x_scales, w1, w2, e_words, e_scales, unit, prior, offs, ent, cor, out
):
    nc = tc.nc
    with ExitStack() as ctx:
        sb = ctx.enter_context(tc.tile_pool(name="sb", bufs=1))
        ps = ctx.enter_context(tc.psum_pool(name="ps", bufs=1))

        offs_t = sb.tile([P, S // 16], U16, name="offs_t")
        ent_t = sb.tile([P, Z // 16], U16, name="ent_t")
        cor_t = sb.tile([P, V // 16], U16, name="cor_t")
        x_tab = sb.tile([P, T], U32, name="x_tab", tag="x_tab", align_bytes=64)
        e_tab = sb.tile([P, T], U32, name="e_tab")
        xs_tab = sb.tile([P, T], U8, name="xs_tab")
        es_tab = sb.tile([P, T], U8, name="es_tab")
        w1_raw = sb.tile([P, PACK, H], F32, name="w1_raw")
        w2_raw = [sb.tile([P, PACK, H // 2], F32, name="w2_raw%d" % a, tag="w2_raw%d" % a) for a in range(2)]
        prior_col = sb.tile([P, T // P], F32, name="prior_col")
        unit_t = sb.tile([P, PACK], F32, name="unit_t")
        ident = sb.tile([P, P], F32, name="ident")
        counts = sb.tile([P, TERMS + 1], F32, name="counts")
        log_counts = sb.tile([P, TERMS], F32, name="log_counts")

        nc.vector.memset(xs_tab[:].bitcast(I32), 0)
        nc.vector.memset(es_tab[:].bitcast(I32), 0)
        nc.gpsimd.iota(counts[:], [[-1, TERMS + 1]], base=TERMS, channel_multiplier=0, allow_small_or_imprecise_dtypes=True)
        make_identity(nc, ident[:])

        w1_rows = w1.rearrange("(p j) c -> p j c", j=PACK)
        w2_rows = w2.rearrange("(p j) c -> p j c", j=PACK)
        nc.sync.dma_start(out=prior_col[:], in_=prior[0, :].rearrange("(n b) -> n b", b=T // P))
        nc.sync.dma_start(offs_t[:], offs)
        nc.sync.dma_start(ent_t[:], ent)
        nc.sync.dma_start(cor_t[:], cor)
        for j in range(PACK):
            nc.sync.dma_start(out=w1_raw[:, j, :], in_=w1_rows[:, j, :])
        load_scale_rows(nc.sync, xs_tab, x_scales)
        nc.sync.dma_start(out=x_tab[:].bitcast(I32), in_=x_words[0].rearrange("p n r -> p (n r)").bitcast(I32))
        load_scale_rows(nc.sync, es_tab, e_scales)
        for a in range(2):
            nc.sync.dma_start(out=w2_raw[a][:], in_=w2_rows[:, :, a * (H // 2) : (a + 1) * (H // 2)])
        nc.sync.dma_start(out=unit_t[:], in_=unit.rearrange("(p t) o -> p (t o)", t=PACK))
        nc.sync.dma_start(out=e_tab[:].bitcast(I32), in_=e_words[0].rearrange("p n r -> p (n r)").bitcast(I32))

        nc.scalar.activation(log_counts[:], counts[:, 0:TERMS], ACT.Ln)

        log_prior = sb.tile([P, T], F32, name="log_prior")
        log_prior_v = log_prior[:].rearrange("p (n b) -> p n b", b=T // P)
        for q in range(4):
            spread = ps.tile([P, 4, P], F32, name="spread%d" % q, tag="bank_a%d" % q)
            for i in range(4):
                b = 4 * q + i
                nc.tensor.transpose(spread[:, i, :], prior_col[:, b : b + 1].to_broadcast([P, P]), ident[:])
            nc.scalar.activation(
                log_prior_v[:, :, 4 * q : 4 * q + 4], spread[:].rearrange("p i n -> p n i"), ACT.Ln
            )

        x_codes = sb.tile([P, S], U32, name="x_codes", align_bytes=64)
        x_bytes = sb.tile([P, S], U8, name="x_bytes", align_bytes=64)
        w_bf = [sb.tile([P, PACK, P, PACK], BF16, name="w_bf%d" % n, align_bytes=64) for n in range(2)]
        w_codes = [sb.tile([P, H], U32, name="w_codes%d" % n, align_bytes=64) for n in range(2)]
        w_bytes = [sb.tile([P, H], U8, name="w_bytes%d" % n, align_bytes=64) for n in range(2)]

        def deal(copy, dealt, raw):
            copy(out=dealt.rearrange("p t m j -> p m j t"), in_=raw.rearrange("p j (m t) -> p m j t", t=PACK))

        def quantize_weights(n, t):
            cols = slice(t * P, (t + 1) * P)
            nc.vector.quantize_mx(
                out=w_codes[n][:, cols].bitcast(FP8X4),
                scales=w_bytes[n][:, cols],
                in_=w_bf[n][:, t].rearrange("p m j -> p (m j)"),
            )

        def first_product(n, t, bank):
            cols = slice(t * P, (t + 1) * P)
            nc.tensor.matmul_mx(
                out=bank[:],
                lhsT=w_codes[n][:, cols].bitcast(FP8X4),
                lhsT_scale=w_bytes[n][:, cols],
                rhs=x_codes[:].bitcast(FP8X4),
                rhs_scale=x_bytes[:],
                start=True,
                stop=True,
            )

        ent_prior = sb.tile([P, Z], F32, name="ent_prior")
        nc.scalar.activation(ent_prior[:], log_prior[:].indirect(ent_t[:]), ACT.Copy)
        deal(nc.vector.tensor_copy, w_bf[0][:], w1_raw[:])
        for t in range(PACK):
            quantize_weights(0, t)
        nc.vector.tensor_copy(x_bytes[:], xs_tab[:].indirect(offs_t[:]))
        nc.vector.tensor_copy(x_codes[:], x_tab[:].indirect(offs_t[:]))
        e_bytes = sb.tile([P, Z], U8, name="e_bytes", tag="x_tab", align_bytes=64)
        nc.vector.tensor_copy(e_bytes[:], es_tab[:].indirect(ent_t[:]))
        deal(nc.scalar.copy, w_bf[1][:, :, 0 : P // 2, :], w2_raw[0][:])
        relu_y = sb.tile([P, PACK, S], F32, name="relu_y", tag="w2_raw0")
        for t in range(PACK):
            y = ps.tile([P, S], F32, name="y%d" % t, tag="bank_a%d" % t)
            first_product(0, t, y)
            nc.scalar.activation(relu_y[:, t, :], y[:], ACT.Relu)
        deal(nc.vector.tensor_copy, w_bf[1][:, :, P // 2 : P, :], w2_raw[1][:])
        yw = []
        for t in range(PACK):
            quantize_weights(1, t)
            bank = ps.tile([P, S], F32, name="yw%d" % t, tag="bank_b%d" % t)
            first_product(1, t, bank)
            yw.append(bank)

        yr = [sb.tile([P, V, 2], F32, name="yr%d" % t, tag="yr%d" % t, align_bytes=64) for t in range(PACK)]
        ment = [sb.tile([P, V], F32, name="ment%d" % t, tag="ment%d" % t) for t in range(PACK)]
        gate = sb.tile([P, PACK, V], F32, name="gate")
        scaled = sb.tile([P, PACK, V], F32, name="scaled")

        def difference(t):
            nc.vector.scalar_tensor_tensor(
                yr[t][:].rearrange("p v d -> p (v d)"), yw[t][:], -0.5, relu_y[:, t, :], ALU.mult, ALU.add
            )

        def mention(t):
            nc.vector.tensor_tensor(ment[t][:], yr[t][:, :, 0], yr[t][:, :, 1], ALU.max)
            for h in range(2):
                nc.scalar.activation(
                    gate[:, t, h * P : (h + 1) * P], ment[t][:].indirect(cor_t[:, h * 8 : (h + 1) * 8]), ACT.Sigmoid
                )
            nc.gpsimd.tensor_scalar(scaled[:, t, :], ment[t][:], unit_t[:, t : t + 1], 0.0, ALU.mult, ALU.add)

        difference(0)
        for t in range(1, PACK):
            difference(t)
            mention(t - 1)
        mention(PACK - 1)
        e_codes = sb.tile([P, Z], U32, name="e_codes", tag="yr%d" % (PACK - 1), align_bytes=64)
        nc.vector.tensor_copy(e_codes[:], e_tab[:].indirect(ent_t[:]))
        coefs = sb.tile([P, TERMS + 1], F32, name="coefs", tag="ment%d" % (PACK - 1))
        nc.scalar.activation(coefs[:, 0:TERMS], log_counts[:], ACT.Exp, scale=-1.0)
        nc.gpsimd.tensor_scalar(
            coefs[:, TERMS : TERMS + 1], counts[:, TERMS : TERMS + 1], 1.0, -math.log(CENTRE), ALU.mult, ALU.add
        )

        hid = [sb.tile([P, P, PACK], BF16, name="hid%d" % h, align_bytes=64) for h in range(2)]
        sc = [ps.tile([P, Z], F32, name="sc%d" % h, tag="bank_a%d" % h) for h in range(2)]
        lp = [sb.tile([P, Z], F32, name="lp%d" % h) for h in range(2)]

        def hidden(h):
            rows = slice(h * P, (h + 1) * P)
            nc.vector.tensor_tensor(
                hid[h][:].rearrange("p (c i) t -> p c t i", i=4),
                gate[:, :, rows].rearrange("p t (c i) -> p c t i", i=4),
                scaled[:, :, rows].rearrange("p t (c i) -> p c t i", i=4),
                ALU.mult,
            )

        def second_product(h):
            hid_codes = sb.tile([P, P], U32, name="hid_codes%d" % h, align_bytes=64)
            hid_bytes = sb.tile([P, P], U8, name="hid_bytes%d" % h, align_bytes=64)
            nc.vector.quantize_mx(
                out=hid_codes[:].bitcast(FP8X4), scales=hid_bytes[:], in_=hid[h][:].rearrange("p v t -> p (v t)")
            )
            nc.tensor.matmul_mx(
                out=sc[h][:],
                lhsT=hid_codes[:].bitcast(FP8X4),
                lhsT_scale=hid_bytes[:],
                rhs=e_codes[:].bitcast(FP8X4),
                rhs_scale=e_bytes[:],
                start=True,
                stop=True,
            )

        hidden(0)
        second_product(0)
        hidden(1)
        nc.vector.tensor_tensor(lp[0][:], sc[0][:], ent_prior[:], ALU.add)
        second_product(1)
        nc.vector.tensor_tensor(lp[1][:], sc[1][:], ent_prior[:], ALU.add)

        for h in range(2):
            rows = slice(h * P, (h + 1) * P)
            squashed = sb.tile([P, Z], F32, name="squashed%d" % h)
            el = sb.tile([P, Z], F32, name="el%d" % h)
            total = sb.tile([P, 1], F32, name="total%d" % h)
            below = sb.tile([P, 1], F32, name="below%d" % h)
            series = sb.tile([P, TERMS + 1], F32, name="series%d" % h)
            over = sb.tile([P, Z], F32, name="over%d" % h)
            result = sb.tile([P, Z], F32, name="result%d" % h)
            nc.scalar.activation(squashed[:], lp[h][:], ACT.Tanh)
            nc.scalar.activation(el[:], squashed[:], ACT.Exp, scale=2.0, accum_out=total[:])
            if h == 0:
                nc.vector.tensor_scalar(below[:], total[:], -1.0 / (Z * CENTRE), 1.0 - 0.05 / CENTRE, ALU.mult, ALU.add)
            else:
                nc.scalar.activation(below[:], total[:], ACT.Copy, scale=-1.0 / (Z * CENTRE), bias=1.0 - 0.05 / CENTRE)
            nc.vector.tensor_tensor_scan(
                series[:], below[:].to_broadcast([P, TERMS + 1]), coefs[:], 0.0, ALU.mult, ALU.add
            )
            minus_lse = series[:, TERMS : TERMS + 1]
            if h == 0:
                nc.vector.tensor_scalar(over[:], lp[h][:], minus_lse, 0.0, ALU.add, ALU.max)
                nc.vector.tensor_tensor(result[:], sc[h][:], over[:], ALU.mult)
                nc.sync.dma_start(out=out[rows, :], in_=result[:])
            else:
                left, right = slice(0, Z // 2), slice(Z // 2, Z)
                nc.vector.tensor_scalar(over[:, left], lp[h][:, left], minus_lse, 0.0, ALU.add, ALU.max)
                nc.scalar.activation(over[:, right], lp[h][:, right], ACT.Relu, bias=minus_lse)
                for cols, queue in ((left, nc.sync), (right, nc.scalar)):
                    nc.vector.tensor_tensor(result[:, cols], sc[h][:, cols], over[:, cols], ALU.mult)
                    queue.dma_start(out=out[rows, cols], in_=result[:, cols])
